import numpy as np
import ml_dtypes


def mxq(x, axis, fmt="e4m3"):
    dtype, down = {"e4m3": (ml_dtypes.float8_e4m3fn, 7), "e5m2": (ml_dtypes.float8_e5m2, 14)}[fmt]
    v = np.moveaxis(np.asarray(x, np.float32).astype(ml_dtypes.bfloat16).astype(np.float64), axis, -1)
    blocks = v.reshape(v.shape[:-1] + (-1, 32))
    amax = np.abs(blocks).max(-1, keepdims=True)
    byte = np.maximum(np.where(amax > 0, np.frexp(amax)[1] - 1 + 127, 0) - down, 1)
    scale = np.exp2(byte - 127.0)
    codes = (blocks / scale).astype(np.float32).astype(dtype).astype(np.float64)
    return np.moveaxis((codes * scale).reshape(v.shape), -1, axis)


WIDE = False


def mx_kscale(k):
    if not WIDE:
        return np.ones(k)
    levels = np.array([10, -10, 5, -5, 0])
    if k % 512:
        return np.exp2(np.random.permutation(np.resize(levels, k // 32))).repeat(32)
    a = np.empty((k // 512, 16))
    for p in range(k // 512):
        a[p, :8] = np.random.permutation(np.resize(levels, 8))
        for g in range(8):
            far = levels[np.abs(levels - a[p, g]) >= 10]
            a[p, g + 8] = far[np.random.randint(len(far))]
    return np.exp2(a.ravel()).repeat(32)


def f64(x):
    return np.asarray(x).astype(np.float64)


def striped(idx):
    return np.tile(idx.reshape(-1, 16).T, (8, 1)).astype(np.uint16)


def unstriped(offs):
    return offs[:16].T.reshape(-1).astype(np.int64)


def striped8(idx):
    return np.concatenate([x.reshape(-1, 16).T for x in idx]).astype(np.uint16)


def runs(offs, k):
    lists = np.stack([offs[16 * r : 16 * r + 16].T.reshape(-1) for r in range(8)]).astype(np.int64)
    return lists[np.arange(k) % 512 // 64]


def pack_weight(w):
    k, n = w.shape
    w = f64(np.asarray(w, np.float32).astype(ml_dtypes.bfloat16)).reshape(k // 32, 32, n)
    amax = np.abs(w).max(1)
    byte = np.clip(np.where(amax > 0, np.frexp(amax)[1] - 1 + 127 - 7, 1), 1, 254)
    scaled = (w * np.exp2(127.0 - byte)[:, None, :]).reshape(k, n).astype(np.float32)
    words = np.ascontiguousarray(scaled.reshape(k // 512, 128, 4, n).transpose(0, 1, 3, 2)).astype(ml_dtypes.float8_e4m3fn).view(np.uint8)
    return words, np.ascontiguousarray(byte.astype(np.uint8).reshape(k // 512, 16, n))


def unpack_weight(words, scales):
    g, p, n, _ = words.shape
    vals = np.ascontiguousarray(words).view(ml_dtypes.float8_e4m3fn).astype(np.float64) * np.repeat(np.exp2(scales.astype(np.float64) - 127.0), 8, axis=1)[..., None]
    return vals.transpose(0, 1, 3, 2).reshape(g * 512, n)


def sigmoid(v):
    return 1.0 / (1.0 + np.exp(-np.maximum(v, -700.0)))


K, T, S, N, G, H = 512, 1024, 256, 512, 2048, 512


def setup_inputs():
    n = np.random.standard_normal
    s = mx_kscale(K)[:, None]
    u = mx_kscale(K)
    packed_xT = pack_weight(n((K, T)) * s)
    packed_dT = pack_weight(n((K, G)) / s)
    return {
        "x_words": packed_xT[0],
        "x_scales": packed_xT[1],
        "d_words": packed_dT[0],
        "d_scales": packed_dT[1],
        "sl": np.random.uniform(1.0, 2.0, (H, 1)).astype(np.float32),
        "th": (0.5 * n((H, 1))).astype(np.float32),
        "gn": (np.random.uniform(0.5, 1.5, (H, 1)) * u[:, None]).astype(np.float32),
        "w1": (n((H, N)) / np.sqrt(2 * H) / u[:, None]).astype(np.float32),
        "w2": (n((K, N)) / np.sqrt(2 * K) / s).astype(np.float32),
        "offs": striped(np.random.permutation(T)[:S]),
        "ci": striped(np.random.permutation(G)[:H]),
        "n1": striped8(np.stack([np.random.permutation(S) for _ in range(8)])),
        "n2": striped8(np.stack([np.random.permutation(S) for _ in range(8)])),
        "two": striped(np.random.permutation(T)[:S]),
        "n3": striped(np.random.permutation(S)),
    }


def reference(x_words, x_scales, d_words, d_scales, sl, th, gn, w1, w2, offs, ci, n1, n2, two, n3):
    d_ci = unpack_weight(d_words, d_scales)[:, unstriped(ci)]
    xq = unpack_weight(x_words, x_scales)[:, unstriped(offs)]
    s = 0.0625 * (d_ci.T @ xq)
    pa = s[np.arange(H)[:, None], runs(n1, H)]
    sg = sigmoid(f64(sl) * (s[np.arange(H)[:, None], runs(n2, H)] - f64(th)))
    z = f64(gn) * (pa + sg * (s - pa))
    x_two = unpack_weight(x_words, x_scales)[:, unstriped(two)]
    h = mxq(f64(w1), 0, "e4m3").T @ mxq(z, 0, "e4m3") + mxq(f64(w2), 0, "e4m3").T @ x_two
    ds = np.zeros((N, S))
    ds[:, unstriped(n3)] = h
    return h - ds

@@ -1,0 +1,224 @@
+from contextlib import ExitStack
+
+import concourse.mybir as mybir
+
+K, T, S, N, G, H = 512, 1024, 256, 512, 2048, 512
+FLOPS = 2 * K * H * S + 2 * H * N * S + 2 * K * N * S
+
+F32 = mybir.dt.float32
+BF16 = mybir.dt.bfloat16
+I32 = mybir.dt.int32
+U32 = mybir.dt.uint32
+U16 = mybir.dt.uint16
+U8 = mybir.dt.uint8
+FP8X4 = mybir.dt.float8_e4m3fn_x4
+ACT = mybir.ActivationFunctionType
+ALU = mybir.AluOpType
+
+P = 128
+PACK = 4
+HALF = S // 2
+
+
+def tile_picked_dwmeblsendmx_none_p_kernel(
+    tc, x_words, x_scales, d_words, d_scales, sl, th, gn, w1, w2, offs, ci, n1, n2, two, n3, out
+):
+    nc = tc.nc
+    with ExitStack() as ctx:
+        sb = ctx.enter_context(tc.tile_pool(name="sb", bufs=1))
+        shared = ctx.enter_context(tc.tile_pool(name="shared", bufs=1))
+        ps = ctx.enter_context(tc.psum_pool(name="ps", bufs=1))
+
+        def load_list(src, name):
+            dst = sb.tile(list(src.shape), U16, name=name)
+            nc.sync.dma_start(dst[:], src)
+            return dst
+
+        def load_column(src, name):
+            dst = sb.tile([P, PACK], F32, name=name)
+            nc.sync.dma_start(dst[:], src.rearrange("(p t) o -> p (t o)", t=PACK))
+            return dst
+
+        def load_scales(src, name):
+            table = sb.tile([P, src.shape[2]], U8, name=name)
+            for q in range(4):
+                rows = src[0, 4 * q : 4 * q + 4, :].bitcast(I32)
+                nc.sync.dma_start(
+                    table[32 * q : 32 * q + 32, :].bitcast(I32), rows.unsqueeze(0).to_broadcast([8, 4, src.shape[2] // 4])
+                )
+            return table
+
+        def load_words(src, name):
+            table = sb.tile([P, src.shape[2]], U32, name=name)
+            nc.sync.dma_start(table[:].bitcast(I32), src[0].rearrange("p n t -> p (n t)").bitcast(I32))
+            return table
+
+        def load_w(src, c, raw):
+            nc.sync.dma_start(raw[:], src.rearrange("(p j) m -> p j m", j=PACK)[:, :, c * (N // 2) : (c + 1) * (N // 2)])
+            return raw
+
+        warm_in = sb.tile([P, 1], F32, name="warm_in")
+        warm_out = sb.tile([P, 1], F32, name="warm_out")
+        nc.gpsimd.memset(warm_in[:], 0.0)
+        nc.scalar.activation(out=warm_out[:], in_=warm_in[:], func=ACT.Sigmoid)
+
+        offs_l = load_list(offs, "offs_l")
+        x_scale_table = load_scales(x_scales, "x_scale_table")
+        two_l = load_list(two, "two_l")
+        x_table = load_words(x_words, "x_table")
+        d_table = load_words(d_words, "d_table")
+        ci_l = load_list(ci, "ci_l")
+        d_scale_table = load_scales(d_scales, "d_scale_table")
+        sl_t = load_column(sl, "sl_t")
+        w2_lo = load_w(w2, 0, shared.tile([P, PACK, N // 2], F32, name="w2_lo", offset=0))
+        w1_lo = load_w(w1, 0, sb.tile([P, PACK, N // 2], F32, name="w1_lo"))
+        th_t = load_column(th, "th_t")
+        n1_l = load_list(n1, "n1_l")
+        n2_l = load_list(n2, "n2_l")
+        gn_t = load_column(gn, "gn_t")
+        w2_hi = load_w(w2, 1, sb.tile([P, PACK, N // 2], F32, name="w2_hi"))
+        w1_hi = load_w(w1, 1, sb.tile([P, PACK, N // 2], F32, name="w1_hi"))
+        n3_l = load_list(n3, "n3_l")
+
+        def interleave(copy, grouped, planes):
+            copy(grouped.rearrange("p (c i) j -> p c j i", i=4), planes.rearrange("p j (c i) -> p c j i", i=4))
+
+        def quantize(codes, scale, grouped):
+            nc.vector.quantize_mx(out=codes.bitcast(FP8X4), scales=scale, in_=grouped.rearrange("p c j -> p (c j)"))
+
+        d_scale = sb.tile([P, H], U8, name="d_scale", align_bytes=64)
+        d_codes = sb.tile([P, H], U32, name="d_codes", align_bytes=64)
+        x_scale = sb.tile([P, S], U8, name="x_scale", align_bytes=64)
+        x_codes = sb.tile([P, S], U32, name="x_codes", align_bytes=64)
+        y_scale = sb.tile([P, S], U8, name="y_scale", align_bytes=64)
+        y_codes = sb.tile([P, S], U32, name="y_codes", align_bytes=64)
+        nc.vector.tensor_copy(x_scale[:], x_scale_table[:].indirect(offs_l[:]))
+        nc.vector.tensor_copy(y_scale[:], x_scale_table[:].indirect(two_l[:]))
+        nc.vector.tensor_copy(x_codes[:], x_table[:].indirect(offs_l[:]))
+        nc.vector.tensor_copy(y_codes[:], x_table[:].indirect(two_l[:]))
+        nc.vector.tensor_copy(d_codes[:].rearrange("p (t m) -> p m t", t=PACK), d_table[:].indirect(ci_l[:]))
+        nc.vector.tensor_copy(d_scale[:].rearrange("p (t m) -> p m t", t=PACK), d_scale_table[:].indirect(ci_l[:]))
+
+        bias = sb.tile([P, PACK], F32, name="bias")
+        nc.vector.scalar_tensor_tensor(bias[:], sl_t[:], -1.0, th_t[:], ALU.mult, ALU.mult)
+
+        w2_lo_bf = sb.tile([P, N // 2, PACK], BF16, name="w2_lo_bf", align_bytes=64)
+        interleave(nc.scalar.copy, w2_lo_bf[:], w2_lo[:])
+
+        s_row = []
+        for t in range(PACK):
+            bank = ps.tile([P, S], F32, name="s_bank%d" % t, tag="bank%d" % t)
+            nc.tensor.matmul_mx(
+                out=bank[:],
+                lhsT=d_codes[:, t * P : (t + 1) * P].bitcast(FP8X4),
+                lhsT_scale=d_scale[:, t * P : (t + 1) * P],
+                rhs=x_codes[:].bitcast(FP8X4),
+                rhs_scale=x_scale[:],
+                start=True,
+                stop=True,
+            )
+            row = shared.tile([P, S], F32, name="s_row%d" % t, offset=4 * S * t)
+            nc.scalar.activation(out=row[:], in_=bank[:], func=ACT.Copy, scale=0.0625)
+            s_row.append(row)
+
+        def look_up(u):
+            lists = slice(u * HALF // 16, (u + 1) * HALF // 16)
+            sg = sb.tile([P, PACK, HALF], F32, name="sg%d" % u)
+            pa = sb.tile([P, PACK, HALF], F32, name="pa%d" % u)
+            for t in range(PACK):
+                nc.scalar.activation(out=pa[:, t, :], in_=s_row[t][:].indirect(n1_l[:, lists]), func=ACT.Copy)
+                nc.scalar.activation(
+                    out=sg[:, t, :],
+                    in_=s_row[t][:].indirect(n2_l[:, lists]),
+                    func=ACT.Sigmoid,
+                    scale=sl_t[:, t : t + 1],
+                    bias=bias[:, t : t + 1],
+                )
+            return pa, sg
+
+        looked_up = [look_up(u) for u in range(2)]
+
+        w_mx = {}
+        w1_lo_bf = sb.tile([P, N // 2, PACK], BF16, name="w1_lo_bf", tag="diff0", align_bytes=64)
+        interleave(nc.vector.tensor_copy, w1_lo_bf[:], w1_lo[:])
+        for name, grouped in (("w2", w2_lo_bf), ("w1", w1_lo_bf)):
+            codes = sb.tile([P, N // 2], U32, name=name + "_lo_codes", align_bytes=64)
+            scale = sb.tile([P, N // 2], U8, name=name + "_lo_scale", align_bytes=64)
+            quantize(codes[:], scale[:], grouped[:])
+            for m in range(2):
+                w_mx[name, m] = (codes[:, m * P : (m + 1) * P], scale[:, m * P : (m + 1) * P])
+
+        def prepare_hi(m, tag):
+            cols = slice((m - 2) * P, (m - 1) * P)
+            grouped = sb.tile([P, 2 * P, PACK], BF16, name="w_bf%d" % m, tag=tag, align_bytes=64)
+            interleave(nc.vector.tensor_copy, grouped[:, 0:P, :], w2_hi[:, :, cols])
+            interleave(nc.vector.tensor_copy, grouped[:, P : 2 * P, :], w1_hi[:, :, cols])
+            codes = sb.tile([P, 2 * P], U32, name="w_codes%d" % m, align_bytes=64)
+            scale = sb.tile([P, 2 * P], U8, name="w_scale%d" % m, align_bytes=64)
+            quantize(codes[:], scale[:], grouped[:])
+            w_mx["w2", m] = (codes[:, 0:P], scale[:, 0:P])
+            w_mx["w1", m] = (codes[:, P : 2 * P], scale[:, P : 2 * P])
+
+        z_codes = sb.tile([P, S], U32, name="z_codes", align_bytes=64)
+        z_scale = sb.tile([P, S], U8, name="z_scale", align_bytes=64)
+
+        def make_z(u):
+            cols = slice(u * HALF, (u + 1) * HALF)
+            pa, sg = looked_up[u]
+            diff = sb.tile([P, PACK, HALF], F32, name="diff%d" % u, tag="diff%d" % u, align_bytes=64)
+            gated = sb.tile([P, PACK, HALF], F32, name="gated%d" % u, tag="gated%d" % u, align_bytes=64)
+            z = sb.tile([P, PACK, HALF], F32, name="z%d" % u, tag="z%d" % u, align_bytes=64)
+            for t in range(PACK):
+                nc.vector.tensor_tensor(diff[:, t, :], s_row[t][:, cols], pa[:, t, :], ALU.subtract)
+                nc.vector.scalar_tensor_tensor(gated[:, t, :], diff[:, t, :], gn_t[:, t : t + 1], sg[:, t, :], ALU.mult, ALU.mult)
+                nc.vector.scalar_tensor_tensor(z[:, t, :], pa[:, t, :], gn_t[:, t : t + 1], gated[:, t, :], ALU.mult, ALU.add)
+            grouped = sb.tile([P, HALF, PACK], BF16, name="z_bf%d" % u, align_bytes=64)
+            interleave(nc.vector.tensor_copy, grouped[:], z[:])
+            quantize(z_codes[:, cols], z_scale[:, cols], grouped[:])
+
+        last = N // P - 1
+        h_row = [sb.tile([P, S], F32, name="h_row%d" % m) for m in range(N // P)]
+        ds = [sb.tile([P, 2 * S if m == last else S], F32, name="ds%d" % m) for m in range(N // P)]
+
+        def make_h(m, first, width, tag):
+            cols = slice(first, first + width)
+            bank = ps.tile([P, width], F32, name="h_bank%d_%d" % (m, first), tag=tag)
+            nc.tensor.matmul_mx(
+                out=bank[:],
+                lhsT=w_mx["w2", m][0].bitcast(FP8X4),
+                lhsT_scale=w_mx["w2", m][1],
+                rhs=y_codes[:, cols].bitcast(FP8X4),
+                rhs_scale=y_scale[:, cols],
+                start=True,
+                stop=False,
+            )
+            nc.tensor.matmul_mx(
+                out=bank[:],
+                lhsT=w_mx["w1", m][0].bitcast(FP8X4),
+                lhsT_scale=w_mx["w1", m][1],
+                rhs=z_codes[:, cols].bitcast(FP8X4),
+                rhs_scale=z_scale[:, cols],
+                start=False,
+                stop=True,
+            )
+            nc.vector.tensor_copy(h_row[m][:, cols], bank[:])
+            nc.scalar.activation(
+                out=ds[m][:].indirect(n3_l[:, first // 16 : (first + width) // 16]), in_=h_row[m][:, cols], func=ACT.Copy
+            )
+
+        make_z(0)
+        for m in range(2):
+            make_h(m, 0, HALF, "bank%d" % (PACK + m))
+        prepare_hi(2, "w_bf2")
+        make_h(2, 0, HALF, "bank6")
+        make_z(1)
+        for m in range(last):
+            make_h(m, HALF, HALF, "bank%d" % m)
+        prepare_hi(last, "z1")
+        make_h(last, 0, S, "bank7")
+        for m in range(last):
+            res = sb.tile([P, S], F32, name="res%d" % m)
+            nc.gpsimd.tensor_tensor(res[:], h_row[m][:], ds[m][:], ALU.subtract)
+            nc.sync.dma_start(out[m * P : (m + 1) * P, :], res[:])
+        nc.vector.tensor_tensor(ds[last][:, S : 2 * S], h_row[last][:], ds[last][:, 0:S], ALU.subtract)
+        nc.sync.dma_start(out[last * P : (last + 1) * P, :], ds[last][:, S : 2 * S])

@@ -26,7 +26,6 @@ def tile_picked_dwmeblsendmx_none_p_kernel(
     nc = tc.nc
     with ExitStack() as ctx:
         sb = ctx.enter_context(tc.tile_pool(name="sb", bufs=1))
-        shared = ctx.enter_context(tc.tile_pool(name="shared", bufs=1))
         ps = ctx.enter_context(tc.psum_pool(name="ps", bufs=1))
 
         def load_list(src, name):
@@ -48,6 +47,13 @@ def tile_picked_dwmeblsendmx_none_p_kernel(
                 )
             return table
 
+        def load_scale_rows(src, name):
+            table = sb.tile([P, src.shape[2]], U8, name=name)
+            nc.gpsimd.memset(table[:].bitcast(I32), 0)
+            for q in range(4):
+                nc.sync.dma_start(table[32 * q : 32 * q + 4, :].bitcast(I32), src[0, 4 * q : 4 * q + 4, :].bitcast(I32))
+            return table
+
         def load_words(src, name):
             table = sb.tile([P, src.shape[2]], U32, name=name)
             nc.sync.dma_start(table[:].bitcast(I32), src[0].rearrange("p n t -> p (n t)").bitcast(I32))
@@ -66,15 +72,15 @@ def tile_picked_dwmeblsendmx_none_p_kernel(
         x_scale_table = load_scales(x_scales, "x_scale_table")
         two_l = load_list(two, "two_l")
         x_table = load_words(x_words, "x_table")
-        d_table = load_words(d_words, "d_table")
         ci_l = load_list(ci, "ci_l")
-        d_scale_table = load_scales(d_scales, "d_scale_table")
+        d_scale_table = load_scale_rows(d_scales, "d_scale_table")
+        d_table = load_words(d_words, "d_table")
         sl_t = load_column(sl, "sl_t")
-        w2_lo = load_w(w2, 0, shared.tile([P, PACK, N // 2], F32, name="w2_lo", offset=0))
-        w1_lo = load_w(w1, 0, sb.tile([P, PACK, N // 2], F32, name="w1_lo"))
         th_t = load_column(th, "th_t")
         n1_l = load_list(n1, "n1_l")
         n2_l = load_list(n2, "n2_l")
+        w2_lo = load_w(w2, 0, sb.tile([P, PACK, N // 2], F32, name="w2_lo"))
+        w1_lo = load_w(w1, 0, sb.tile([P, PACK, N // 2], F32, name="w1_lo"))
         gn_t = load_column(gn, "gn_t")
         w2_hi = load_w(w2, 1, sb.tile([P, PACK, N // 2], F32, name="w2_hi"))
         w1_hi = load_w(w1, 1, sb.tile([P, PACK, N // 2], F32, name="w1_hi"))
@@ -96,14 +102,11 @@ def tile_picked_dwmeblsendmx_none_p_kernel(
         nc.vector.tensor_copy(y_scale[:], x_scale_table[:].indirect(two_l[:]))
         nc.vector.tensor_copy(x_codes[:], x_table[:].indirect(offs_l[:]))
         nc.vector.tensor_copy(y_codes[:], x_table[:].indirect(two_l[:]))
-        nc.vector.tensor_copy(d_codes[:].rearrange("p (t m) -> p m t", t=PACK), d_table[:].indirect(ci_l[:]))
         nc.vector.tensor_copy(d_scale[:].rearrange("p (t m) -> p m t", t=PACK), d_scale_table[:].indirect(ci_l[:]))
+        nc.vector.tensor_copy(d_codes[:].rearrange("p (t m) -> p m t", t=PACK), d_table[:].indirect(ci_l[:]))
 
         bias = sb.tile([P, PACK], F32, name="bias")
         nc.vector.scalar_tensor_tensor(bias[:], sl_t[:], -1.0, th_t[:], ALU.mult, ALU.mult)
-
-        w2_lo_bf = sb.tile([P, N // 2, PACK], BF16, name="w2_lo_bf", align_bytes=64)
-        interleave(nc.scalar.copy, w2_lo_bf[:], w2_lo[:])
 
         s_row = []
         for t in range(PACK):
@@ -117,18 +120,19 @@ def tile_picked_dwmeblsendmx_none_p_kernel(
                 start=True,
                 stop=True,
             )
-            row = shared.tile([P, S], F32, name="s_row%d" % t, offset=4 * S * t)
+            row = sb.tile([P, S], F32, name="s_row%d" % t)
             nc.scalar.activation(out=row[:], in_=bank[:], func=ACT.Copy, scale=0.0625)
             s_row.append(row)
 
         def look_up(u):
             lists = slice(u * HALF // 16, (u + 1) * HALF // 16)
-            sg = sb.tile([P, PACK, HALF], F32, name="sg%d" % u)
-            pa = sb.tile([P, PACK, HALF], F32, name="pa%d" % u)
+            pa, sg = [], []
             for t in range(PACK):
-                nc.scalar.activation(out=pa[:, t, :], in_=s_row[t][:].indirect(n1_l[:, lists]), func=ACT.Copy)
+                pa.append(sb.tile([P, HALF], F32, name="pa%d_%d" % (u, t), tag="pa%d" % t))
+                sg.append(sb.tile([P, HALF], F32, name="sg%d_%d" % (u, t), tag="sg%d" % t))
+                nc.scalar.activation(out=pa[t][:], in_=s_row[t][:].indirect(n1_l[:, lists]), func=ACT.Copy)
                 nc.scalar.activation(
-                    out=sg[:, t, :],
+                    out=sg[t][:],
                     in_=s_row[t][:].indirect(n2_l[:, lists]),
                     func=ACT.Sigmoid,
                     scale=sl_t[:, t : t + 1],
@@ -136,10 +140,12 @@ def tile_picked_dwmeblsendmx_none_p_kernel(
                 )
             return pa, sg
 
-        looked_up = [look_up(u) for u in range(2)]
+        first_look_up = look_up(0)
 
         w_mx = {}
         w1_lo_bf = sb.tile([P, N // 2, PACK], BF16, name="w1_lo_bf", tag="diff0", align_bytes=64)
+        w2_lo_bf = sb.tile([P, N // 2, PACK], BF16, name="w2_lo_bf", align_bytes=64)
+        interleave(nc.vector.tensor_copy, w2_lo_bf[:], w2_lo[:])
         interleave(nc.vector.tensor_copy, w1_lo_bf[:], w1_lo[:])
         for name, grouped in (("w2", w2_lo_bf), ("w1", w1_lo_bf)):
             codes = sb.tile([P, N // 2], U32, name=name + "_lo_codes", align_bytes=64)
@@ -148,12 +154,15 @@ def tile_picked_dwmeblsendmx_none_p_kernel(
             for m in range(2):
                 w_mx[name, m] = (codes[:, m * P : (m + 1) * P], scale[:, m * P : (m + 1) * P])
 
-        def prepare_hi(m, tag):
+        def round_hi(m, copy_w2):
             cols = slice((m - 2) * P, (m - 1) * P)
-            grouped = sb.tile([P, 2 * P, PACK], BF16, name="w_bf%d" % m, tag=tag, align_bytes=64)
-            interleave(nc.vector.tensor_copy, grouped[:, 0:P, :], w2_hi[:, :, cols])
+            grouped = sb.tile([P, 2 * P, PACK], BF16, name="w_bf%d" % m, tag="w_hi_bf", align_bytes=64)
+            interleave(copy_w2, grouped[:, 0:P, :], w2_hi[:, :, cols])
             interleave(nc.vector.tensor_copy, grouped[:, P : 2 * P, :], w1_hi[:, :, cols])
-            codes = sb.tile([P, 2 * P], U32, name="w_codes%d" % m, align_bytes=64)
+            return grouped
+
+        def quantize_hi(m, grouped, tag):
+            codes = sb.tile([P, 2 * P], U32, name="w_codes%d" % m, tag=tag, align_bytes=64)
             scale = sb.tile([P, 2 * P], U8, name="w_scale%d" % m, align_bytes=64)
             quantize(codes[:], scale[:], grouped[:])
             w_mx["w2", m] = (codes[:, 0:P], scale[:, 0:P])
@@ -162,25 +171,27 @@ def tile_picked_dwmeblsendmx_none_p_kernel(
         z_codes = sb.tile([P, S], U32, name="z_codes", align_bytes=64)
         z_scale = sb.tile([P, S], U8, name="z_scale", align_bytes=64)
 
-        def make_z(u):
+        def blend(u, pa, sg):
             cols = slice(u * HALF, (u + 1) * HALF)
-            pa, sg = looked_up[u]
             diff = sb.tile([P, PACK, HALF], F32, name="diff%d" % u, tag="diff%d" % u, align_bytes=64)
             gated = sb.tile([P, PACK, HALF], F32, name="gated%d" % u, tag="gated%d" % u, align_bytes=64)
             z = sb.tile([P, PACK, HALF], F32, name="z%d" % u, tag="z%d" % u, align_bytes=64)
             for t in range(PACK):
-                nc.vector.tensor_tensor(diff[:, t, :], s_row[t][:, cols], pa[:, t, :], ALU.subtract)
-                nc.vector.scalar_tensor_tensor(gated[:, t, :], diff[:, t, :], gn_t[:, t : t + 1], sg[:, t, :], ALU.mult, ALU.mult)
-                nc.vector.scalar_tensor_tensor(z[:, t, :], pa[:, t, :], gn_t[:, t : t + 1], gated[:, t, :], ALU.mult, ALU.add)
-            grouped = sb.tile([P, HALF, PACK], BF16, name="z_bf%d" % u, align_bytes=64)
+                nc.vector.tensor_tensor(diff[:, t, :], s_row[t][:, cols], pa[t][:], ALU.subtract)
+                nc.vector.scalar_tensor_tensor(gated[:, t, :], diff[:, t, :], gn_t[:, t : t + 1], sg[t][:], ALU.mult, ALU.mult)
+                nc.vector.scalar_tensor_tensor(z[:, t, :], pa[t][:], gn_t[:, t : t + 1], gated[:, t, :], ALU.mult, ALU.add)
+            return z
+
+        def quantize_z(u, z):
+            cols = slice(u * HALF, (u + 1) * HALF)
+            grouped = sb.tile([P, HALF, PACK], BF16, name="z_bf%d" % u, tag="z_bf%d" % u, align_bytes=64)
             interleave(nc.vector.tensor_copy, grouped[:], z[:])
             quantize(z_codes[:, cols], z_scale[:, cols], grouped[:])
 
-        last = N // P - 1
         h_row = [sb.tile([P, S], F32, name="h_row%d" % m) for m in range(N // P)]
-        ds = [sb.tile([P, 2 * S if m == last else S], F32, name="ds%d" % m) for m in range(N // P)]
+        ds = [sb.tile([P, S if m < 2 else 2 * S], F32, name="ds%d" % m) for m in range(N // P)]
 
-        def make_h(m, first, width, tag):
+        def make_h(m, first, width, tag, copy):
             cols = slice(first, first + width)
             bank = ps.tile([P, width], F32, name="h_bank%d_%d" % (m, first), tag=tag)
             nc.tensor.matmul_mx(
@@ -201,24 +212,26 @@ def tile_picked_dwmeblsendmx_none_p_kernel(
                 start=False,
                 stop=True,
             )
-            nc.vector.tensor_copy(h_row[m][:, cols], bank[:])
+            copy(h_row[m][:, cols], bank[:])
             nc.scalar.activation(
                 out=ds[m][:].indirect(n3_l[:, first // 16 : (first + width) // 16]), in_=h_row[m][:, cols], func=ACT.Copy
             )
 
-        make_z(0)
+        z_first = blend(0, *first_look_up)
+        second_look_up = look_up(1)
+        quantize_z(0, z_first)
+        w_bf2 = round_hi(2, nc.scalar.copy)
         for m in range(2):
-            make_h(m, 0, HALF, "bank%d" % (PACK + m))
-        prepare_hi(2, "w_bf2")
-        make_h(2, 0, HALF, "bank6")
-        make_z(1)
-        for m in range(last):
-            make_h(m, HALF, HALF, "bank%d" % m)
-        prepare_hi(last, "z1")
-        make_h(last, 0, S, "bank7")
-        for m in range(last):
-            res = sb.tile([P, S], F32, name="res%d" % m)
-            nc.gpsimd.tensor_tensor(res[:], h_row[m][:], ds[m][:], ALU.subtract)
-            nc.sync.dma_start(out[m * P : (m + 1) * P, :], res[:])
-        nc.vector.tensor_tensor(ds[last][:, S : 2 * S], h_row[last][:], ds[last][:, 0:S], ALU.subtract)
-        nc.sync.dma_start(out[last * P : (last + 1) * P, :], ds[last][:, S : 2 * S])
+            make_h(m, 0, HALF, "bank%d" % (PACK + m), nc.scalar.copy)
+        quantize_z(1, blend(1, *second_look_up))
+        for m in range(2):
+            make_h(m, HALF, HALF, "bank%d" % m, nc.vector.tensor_copy)
+        quantize_hi(2, w_bf2, "z_bf1")
+        make_h(2, 0, S, "bank6", nc.vector.tensor_copy)
+        quantize_hi(3, round_hi(3, nc.vector.tensor_copy), "w_codes3")
+        make_h(3, 0, S, "bank7", nc.vector.tensor_copy)
+        for m in range(N // P):
+            res = sb.tile([P, S], F32, name="res%d" % m)[:] if m < 2 else ds[m][:, S : 2 * S]
+            engine = nc.vector if m == N // P - 1 else nc.gpsimd
+            engine.tensor_tensor(res, h_row[m][:], ds[m][:, 0:S], ALU.subtract)
+            nc.sync.dma_start(out[m * P : (m + 1) * P, :], res)

@@ -26,6 +26,7 @@ def tile_picked_dwmeblsendmx_none_p_kernel(
     nc = tc.nc
     with ExitStack() as ctx:
         sb = ctx.enter_context(tc.tile_pool(name="sb", bufs=1))
+        shared = ctx.enter_context(tc.tile_pool(name="shared", bufs=1))
         ps = ctx.enter_context(tc.psum_pool(name="ps", bufs=1))
 
         def load_list(src, name):
@@ -80,7 +81,7 @@ def tile_picked_dwmeblsendmx_none_p_kernel(
         n1_l = load_list(n1, "n1_l")
         n2_l = load_list(n2, "n2_l")
         w2_lo = load_w(w2, 0, sb.tile([P, PACK, N // 2], F32, name="w2_lo"))
-        w1_lo = load_w(w1, 0, sb.tile([P, PACK, N // 2], F32, name="w1_lo"))
+        w1_lo = load_w(w1, 0, shared.tile([P, PACK, N // 2], F32, name="w1_lo", offset=0))
         gn_t = load_column(gn, "gn_t")
         w2_hi = load_w(w2, 1, sb.tile([P, PACK, N // 2], F32, name="w2_hi"))
         w1_hi = load_w(w1, 1, sb.tile([P, PACK, N // 2], F32, name="w1_hi"))
@@ -108,6 +109,11 @@ def tile_picked_dwmeblsendmx_none_p_kernel(
         bias = sb.tile([P, PACK], F32, name="bias")
         nc.vector.scalar_tensor_tensor(bias[:], sl_t[:], -1.0, th_t[:], ALU.mult, ALU.mult)
 
+        w1_lo_bf = sb.tile([P, N // 2, PACK], BF16, name="w1_lo_bf", tag="diff0", align_bytes=64)
+        w2_lo_bf = sb.tile([P, N // 2, PACK], BF16, name="w2_lo_bf", align_bytes=64)
+        interleave(nc.vector.tensor_copy, w2_lo_bf[:], w2_lo[:])
+        interleave(nc.vector.tensor_copy, w1_lo_bf[:], w1_lo[:])
+
         s_row = []
         for t in range(PACK):
             bank = ps.tile([P, S], F32, name="s_bank%d" % t, tag="bank%d" % t)
@@ -120,8 +126,12 @@ def tile_picked_dwmeblsendmx_none_p_kernel(
                 start=True,
                 stop=True,
             )
-            row = sb.tile([P, S], F32, name="s_row%d" % t)
-            nc.scalar.activation(out=row[:], in_=bank[:], func=ACT.Copy, scale=0.0625)
+            if t % 2 == 0:
+                row = sb.tile([P, S], F32, name="s_row%d" % t)
+                nc.scalar.activation(out=row[:], in_=bank[:], func=ACT.Copy, scale=0.0625)
+            else:
+                row = shared.tile([P, S], F32, name="s_row%d" % t, offset=4 * S * (t // 2))
+                nc.vector.tensor_scalar(row[:], bank[:], 0.0625, None, ALU.mult)
             s_row.append(row)
 
         def look_up(u):
@@ -143,10 +153,6 @@ def tile_picked_dwmeblsendmx_none_p_kernel(
         first_look_up = look_up(0)
 
         w_mx = {}
-        w1_lo_bf = sb.tile([P, N // 2, PACK], BF16, name="w1_lo_bf", tag="diff0", align_bytes=64)
-        w2_lo_bf = sb.tile([P, N // 2, PACK], BF16, name="w2_lo_bf", align_bytes=64)
-        interleave(nc.vector.tensor_copy, w2_lo_bf[:], w2_lo[:])
-        interleave(nc.vector.tensor_copy, w1_lo_bf[:], w1_lo[:])
         for name, grouped in (("w2", w2_lo_bf), ("w1", w1_lo_bf)):
             codes = sb.tile([P, N // 2], U32, name=name + "_lo_codes", align_bytes=64)
             scale = sb.tile([P, N // 2], U8, name=name + "_lo_scale", align_bytes=64)
@@ -220,7 +226,7 @@ def tile_picked_dwmeblsendmx_none_p_kernel(
         z_first = blend(0, *first_look_up)
         second_look_up = look_up(1)
         quantize_z(0, z_first)
-        w_bf2 = round_hi(2, nc.scalar.copy)
+        w_bf2 = round_hi(2, nc.vector.tensor_copy)
         for m in range(2):
             make_h(m, 0, HALF, "bank%d" % (PACK + m), nc.scalar.copy)
         quantize_z(1, blend(1, *second_look_up))

from contextlib import ExitStack

import concourse.mybir as mybir

K, T, S, N, G, H = 512, 1024, 256, 512, 2048, 512
FLOPS = 2 * K * H * S + 2 * H * N * S + 2 * K * N * S

F32 = mybir.dt.float32
BF16 = mybir.dt.bfloat16
I32 = mybir.dt.int32
U32 = mybir.dt.uint32
U16 = mybir.dt.uint16
U8 = mybir.dt.uint8
FP8X4 = mybir.dt.float8_e4m3fn_x4
ACT = mybir.ActivationFunctionType
ALU = mybir.AluOpType

P = 128
PACK = 4
HALF = S // 2


def tile_picked_dwmeblsendmx_none_p_kernel(
    tc, x_words, x_scales, d_words, d_scales, sl, th, gn, w1, w2, offs, ci, n1, n2, two, n3, out
):
    nc = tc.nc
    with ExitStack() as ctx:
        sb = ctx.enter_context(tc.tile_pool(name="sb", bufs=1))
        shared = ctx.enter_context(tc.tile_pool(name="shared", bufs=1))
        ps = ctx.enter_context(tc.psum_pool(name="ps", bufs=1))

        def load_list(src, name):
            dst = sb.tile(list(src.shape), U16, name=name)
            nc.sync.dma_start(dst[:], src)
            return dst

        def load_column(src, name):
            dst = sb.tile([P, PACK], F32, name=name)
            nc.sync.dma_start(dst[:], src.rearrange("(p t) o -> p (t o)", t=PACK))
            return dst

        def load_scales(src, name):
            table = sb.tile([P, src.shape[2]], U8, name=name)
            for q in range(4):
                rows = src[0, 4 * q : 4 * q + 4, :].bitcast(I32)
                nc.sync.dma_start(
                    table[32 * q : 32 * q + 32, :].bitcast(I32), rows.unsqueeze(0).to_broadcast([8, 4, src.shape[2] // 4])
                )
            return table

        def load_scale_rows(src, name):
            table = sb.tile([P, src.shape[2]], U8, name=name)
            nc.gpsimd.memset(table[:].bitcast(I32), 0)
            for q in range(4):
                nc.sync.dma_start(table[32 * q : 32 * q + 4, :].bitcast(I32), src[0, 4 * q : 4 * q + 4, :].bitcast(I32))
            return table

        def load_words(src, name):
            table = sb.tile([P, src.shape[2]], U32, name=name)
            nc.sync.dma_start(table[:].bitcast(I32), src[0].rearrange("p n t -> p (n t)").bitcast(I32))
            return table

        def load_w(src, c, raw):
            nc.sync.dma_start(raw[:], src.rearrange("(p j) m -> p j m", j=PACK)[:, :, c * (N // 2) : (c + 1) * (N // 2)])
            return raw

        warm_in = sb.tile([P, 1], F32, name="warm_in")
        warm_out = sb.tile([P, 1], F32, name="warm_out")
        nc.gpsimd.memset(warm_in[:], 0.0)
        nc.scalar.activation(out=warm_out[:], in_=warm_in[:], func=ACT.Sigmoid)

        offs_l = load_list(offs, "offs_l")
        x_scale_table = load_scales(x_scales, "x_scale_table")
        two_l = load_list(two, "two_l")
        x_table = load_words(x_words, "x_table")
        ci_l = load_list(ci, "ci_l")
        d_scale_table = load_scale_rows(d_scales, "d_scale_table")
        d_table = load_words(d_words, "d_table")
        sl_t = load_column(sl, "sl_t")
        th_t = load_column(th, "th_t")
        n1_l = load_list(n1, "n1_l")
        n2_l = load_list(n2, "n2_l")
        w2_lo = load_w(w2, 0, sb.tile([P, PACK, N // 2], F32, name="w2_lo"))
        w1_lo = load_w(w1, 0, shared.tile([P, PACK, N // 2], F32, name="w1_lo", offset=0))
        gn_t = load_column(gn, "gn_t")
        w2_hi = load_w(w2, 1, sb.tile([P, PACK, N // 2], F32, name="w2_hi"))
        w1_hi = load_w(w1, 1, sb.tile([P, PACK, N // 2], F32, name="w1_hi"))
        n3_l = load_list(n3, "n3_l")

        def interleave(copy, grouped, planes):
            copy(grouped.rearrange("p (c i) j -> p c j i", i=4), planes.rearrange("p j (c i) -> p c j i", i=4))

        def quantize(codes, scale, grouped):
            nc.vector.quantize_mx(out=codes.bitcast(FP8X4), scales=scale, in_=grouped.rearrange("p c j -> p (c j)"))

        d_scale = sb.tile([P, H], U8, name="d_scale", align_bytes=64)
        d_codes = sb.tile([P, H], U32, name="d_codes", align_bytes=64)
        x_scale = sb.tile([P, S], U8, name="x_scale", align_bytes=64)
        x_codes = sb.tile([P, S], U32, name="x_codes", align_bytes=64)
        y_scale = sb.tile([P, S], U8, name="y_scale", align_bytes=64)
        y_codes = sb.tile([P, S], U32, name="y_codes", align_bytes=64)
        nc.vector.tensor_copy(x_scale[:], x_scale_table[:].indirect(offs_l[:]))
        nc.vector.tensor_copy(y_scale[:], x_scale_table[:].indirect(two_l[:]))
        nc.vector.tensor_copy(x_codes[:], x_table[:].indirect(offs_l[:]))
        nc.vector.tensor_copy(y_codes[:], x_table[:].indirect(two_l[:]))
        nc.vector.tensor_copy(d_scale[:].rearrange("p (t m) -> p m t", t=PACK), d_scale_table[:].indirect(ci_l[:]))
        nc.vector.tensor_copy(d_codes[:].rearrange("p (t m) -> p m t", t=PACK), d_table[:].indirect(ci_l[:]))

        bias = sb.tile([P, PACK], F32, name="bias")
        nc.vector.scalar_tensor_tensor(bias[:], sl_t[:], -1.0, th_t[:], ALU.mult, ALU.mult)

        w1_lo_bf = sb.tile([P, N // 2, PACK], BF16, name="w1_lo_bf", tag="diff0", align_bytes=64)
        w2_lo_bf = sb.tile([P, N // 2, PACK], BF16, name="w2_lo_bf", align_bytes=64)
        interleave(nc.vector.tensor_copy, w2_lo_bf[:], w2_lo[:])
        interleave(nc.vector.tensor_copy, w1_lo_bf[:], w1_lo[:])

        s_row = []
        for t in range(PACK):
            bank = ps.tile([P, S], F32, name="s_bank%d" % t, tag="bank%d" % t)
            nc.tensor.matmul_mx(
                out=bank[:],
                lhsT=d_codes[:, t * P : (t + 1) * P].bitcast(FP8X4),
                lhsT_scale=d_scale[:, t * P : (t + 1) * P],
                rhs=x_codes[:].bitcast(FP8X4),
                rhs_scale=x_scale[:],
                start=True,
                stop=True,
            )
            if t % 2 == 0:
                row = sb.tile([P, S], F32, name="s_row%d" % t)
                nc.scalar.activation(out=row[:], in_=bank[:], func=ACT.Copy, scale=0.0625)
            else:
                row = shared.tile([P, S], F32, name="s_row%d" % t, offset=4 * S * (t // 2))
                nc.vector.tensor_scalar(row[:], bank[:], 0.0625, None, ALU.mult)
            s_row.append(row)

        def look_up(u):
            lists = slice(u * HALF // 16, (u + 1) * HALF // 16)
            pa, sg = [], []
            for t in range(PACK):
                pa.append(sb.tile([P, HALF], F32, name="pa%d_%d" % (u, t), tag="pa%d" % t))
                sg.append(sb.tile([P, HALF], F32, name="sg%d_%d" % (u, t), tag="sg%d" % t))
                nc.scalar.activation(out=pa[t][:], in_=s_row[t][:].indirect(n1_l[:, lists]), func=ACT.Copy)
                nc.scalar.activation(
                    out=sg[t][:],
                    in_=s_row[t][:].indirect(n2_l[:, lists]),
                    func=ACT.Sigmoid,
                    scale=sl_t[:, t : t + 1],
                    bias=bias[:, t : t + 1],
                )
            return pa, sg

        first_look_up = look_up(0)

        w_mx = {}
        for name, grouped in (("w2", w2_lo_bf), ("w1", w1_lo_bf)):
            codes = sb.tile([P, N // 2], U32, name=name + "_lo_codes", align_bytes=64)
            scale = sb.tile([P, N // 2], U8, name=name + "_lo_scale", align_bytes=64)
            quantize(codes[:], scale[:], grouped[:])
            for m in range(2):
                w_mx[name, m] = (codes[:, m * P : (m + 1) * P], scale[:, m * P : (m + 1) * P])

        def round_hi(m, copy_w2):
            cols = slice((m - 2) * P, (m - 1) * P)
            grouped = sb.tile([P, 2 * P, PACK], BF16, name="w_bf%d" % m, tag="w_hi_bf", align_bytes=64)
            interleave(copy_w2, grouped[:, 0:P, :], w2_hi[:, :, cols])
            interleave(nc.vector.tensor_copy, grouped[:, P : 2 * P, :], w1_hi[:, :, cols])
            return grouped

        def quantize_hi(m, grouped, tag):
            codes = sb.tile([P, 2 * P], U32, name="w_codes%d" % m, tag=tag, align_bytes=64)
            scale = sb.tile([P, 2 * P], U8, name="w_scale%d" % m, align_bytes=64)
            quantize(codes[:], scale[:], grouped[:])
            w_mx["w2", m] = (codes[:, 0:P], scale[:, 0:P])
            w_mx["w1", m] = (codes[:, P : 2 * P], scale[:, P : 2 * P])

        z_codes = sb.tile([P, S], U32, name="z_codes", align_bytes=64)
        z_scale = sb.tile([P, S], U8, name="z_scale", align_bytes=64)

        def blend(u, pa, sg):
            cols = slice(u * HALF, (u + 1) * HALF)
            diff = sb.tile([P, PACK, HALF], F32, name="diff%d" % u, tag="diff%d" % u, align_bytes=64)
            gated = sb.tile([P, PACK, HALF], F32, name="gated%d" % u, tag="gated%d" % u, align_bytes=64)
            z = sb.tile([P, PACK, HALF], F32, name="z%d" % u, tag="z%d" % u, align_bytes=64)
            for t in range(PACK):
                nc.vector.tensor_tensor(diff[:, t, :], s_row[t][:, cols], pa[t][:], ALU.subtract)
                nc.vector.scalar_tensor_tensor(gated[:, t, :], diff[:, t, :], gn_t[:, t : t + 1], sg[t][:], ALU.mult, ALU.mult)
                nc.vector.scalar_tensor_tensor(z[:, t, :], pa[t][:], gn_t[:, t : t + 1], gated[:, t, :], ALU.mult, ALU.add)
            return z

        def quantize_z(u, z):
            cols = slice(u * HALF, (u + 1) * HALF)
            grouped = sb.tile([P, HALF, PACK], BF16, name="z_bf%d" % u, tag="z_bf%d" % u, align_bytes=64)
            interleave(nc.vector.tensor_copy, grouped[:], z[:])
            quantize(z_codes[:, cols], z_scale[:, cols], grouped[:])

        h_row = [sb.tile([P, S], F32, name="h_row%d" % m) for m in range(N // P)]
        ds = [sb.tile([P, S if m < 2 else 2 * S], F32, name="ds%d" % m) for m in range(N // P)]

        def make_h(m, first, width, tag, copy):
            cols = slice(first, first + width)
            bank = ps.tile([P, width], F32, name="h_bank%d_%d" % (m, first), tag=tag)
            nc.tensor.matmul_mx(
                out=bank[:],
                lhsT=w_mx["w2", m][0].bitcast(FP8X4),
                lhsT_scale=w_mx["w2", m][1],
                rhs=y_codes[:, cols].bitcast(FP8X4),
                rhs_scale=y_scale[:, cols],
                start=True,
                stop=False,
            )
            nc.tensor.matmul_mx(
                out=bank[:],
                lhsT=w_mx["w1", m][0].bitcast(FP8X4),
                lhsT_scale=w_mx["w1", m][1],
                rhs=z_codes[:, cols].bitcast(FP8X4),
                rhs_scale=z_scale[:, cols],
                start=False,
                stop=True,
            )
            copy(h_row[m][:, cols], bank[:])
            nc.scalar.activation(
                out=ds[m][:].indirect(n3_l[:, first // 16 : (first + width) // 16]), in_=h_row[m][:, cols], func=ACT.Copy
            )

        z_first = blend(0, *first_look_up)
        second_look_up = look_up(1)
        quantize_z(0, z_first)
        w_bf2 = round_hi(2, nc.vector.tensor_copy)
        for m in range(2):
            make_h(m, 0, HALF, "bank%d" % (PACK + m), nc.scalar.copy)
        quantize_z(1, blend(1, *second_look_up))
        for m in range(2):
            make_h(m, HALF, HALF, "bank%d" % m, nc.vector.tensor_copy)
        quantize_hi(2, w_bf2, "z_bf1")
        make_h(2, 0, S, "bank6", nc.vector.tensor_copy)
        quantize_hi(3, round_hi(3, nc.vector.tensor_copy), "w_codes3")
        make_h(3, 0, S, "bank7", nc.vector.tensor_copy)
        for m in range(N // P):
            res = sb.tile([P, S], F32, name="res%d" % m)[:] if m < 2 else ds[m][:, S : 2 * S]
            engine = nc.vector if m == N // P - 1 else nc.gpsimd
            engine.tensor_tensor(res, h_row[m][:], ds[m][:, 0:S], ALU.subtract)
            nc.sync.dma_start(out[m * P : (m + 1) * P, :], res)
